import numpy as np
import ml_dtypes


def mxq(x, axis, fmt="e4m3"):
    dtype, down = {"e4m3": (ml_dtypes.float8_e4m3fn, 7), "e5m2": (ml_dtypes.float8_e5m2, 14)}[fmt]
    v = np.moveaxis(np.asarray(x, np.float32).astype(ml_dtypes.bfloat16).astype(np.float64), axis, -1)
    blocks = v.reshape(v.shape[:-1] + (-1, 32))
    amax = np.abs(blocks).max(-1, keepdims=True)
    byte = np.maximum(np.where(amax > 0, np.frexp(amax)[1] - 1 + 127, 0) - down, 1)
    scale = np.exp2(byte - 127.0)
    codes = (blocks / scale).astype(np.float32).astype(dtype).astype(np.float64)
    return np.moveaxis((codes * scale).reshape(v.shape), -1, axis)


WIDE = False


def mx_kscale(k):
    if not WIDE:
        return np.ones(k)
    levels = np.array([10, -10, 5, -5, 0])
    if k % 512:
        return np.exp2(np.random.permutation(np.resize(levels, k // 32))).repeat(32)
    a = np.empty((k // 512, 16))
    for p in range(k // 512):
        a[p, :8] = np.random.permutation(np.resize(levels, 8))
        for g in range(8):
            far = levels[np.abs(levels - a[p, g]) >= 10]
            a[p, g + 8] = far[np.random.randint(len(far))]
    return np.exp2(a.ravel()).repeat(32)


def f64(x):
    return np.asarray(x).astype(np.float64)


def striped8(idx):
    return np.asarray(idx).reshape(8, -1, 16).transpose(0, 2, 1).reshape(128, -1).astype(np.uint16)


def unstriped8(offs):
    return offs.reshape(8, 16, -1).transpose(0, 2, 1).reshape(8, -1).astype(np.int64)


def pick8(x, idx, run):
    r = np.arange(len(x))
    return x[r[:, None], idx[r % (8 * run) // run]]


E2M1 = np.array([0.0, 0.5, 1.0, 1.5, 2.0, 3.0, 4.0, 6.0, -0.0, -0.5, -1.0, -1.5, -2.0, -3.0, -4.0, -6.0])


def pack_weight(w, fmt):
    k, n = w.shape
    w = f64(np.asarray(w, np.float32).astype(ml_dtypes.bfloat16)).reshape(k // 32, 32, n)
    amax = np.abs(w).max(1)
    if fmt == "e4m3":
        byte = np.frexp(amax)[1] - 1 + 127 - 7
    else:
        mant, ex = np.frexp(amax / 6.0)
        byte = np.where(mant > 0.5, ex, ex - 1) + 127
    byte = np.clip(np.where(amax > 0, byte, 1), 1, 254)
    scaled = (w * np.exp2(127.0 - byte)[:, None, :]).reshape(k, n).astype(np.float32)
    by_word = np.ascontiguousarray(scaled.reshape(k // 512, 128, 4, n).transpose(0, 1, 3, 2))
    if fmt == "e4m3":
        words = by_word.astype(ml_dtypes.float8_e4m3fn).view(np.uint8)
    else:
        c = by_word.astype(ml_dtypes.float4_e2m1fn).view(np.uint8) & 0xF
        words = (c[..., 0::2] | (c[..., 1::2] << 4)).reshape(k // 512, 128, 2 * n)
    return np.ascontiguousarray(words), np.ascontiguousarray(byte.astype(np.uint8).reshape(k // 512, 16, n))


def unpack_weight(words, scales, fmt):
    g, _, n = scales.shape
    words = np.ascontiguousarray(words).reshape(g, 128, n, -1)
    if fmt == "e4m3":
        vals = words.view(ml_dtypes.float8_e4m3fn).astype(np.float64)
    else:
        nib = np.empty((g, 128, n, 4), np.uint8)
        nib[..., 0::2] = words & 0xF
        nib[..., 1::2] = words >> 4
        vals = E2M1[nib]
    vals = vals * np.repeat(np.exp2(scales.astype(np.float64) - 127.0), 8, axis=1)[..., None]
    return vals.transpose(0, 1, 3, 2).reshape(g * 512, n)


D, T, U, X, I, Q = 512, 1024, 1024, 1024, 512, 128


def setup_inputs():
    n = np.random.standard_normal
    idx = np.stack([np.random.permutation(T)[:I] for _ in range(8)])
    idx2 = np.stack([np.random.permutation(U)[:I] for _ in range(8)])
    idx3 = np.stack([np.random.permutation(X)[:I] for _ in range(8)])
    idx4 = np.stack([np.random.permutation(X)[:I] for _ in range(8)])
    idx5 = np.stack([np.random.permutation(T)[:I] for _ in range(8)])
    idx6 = np.stack([np.random.permutation(T)[:I] for _ in range(8)])
    fd = mx_kscale(D)
    cachep = pack_weight(n((D, T)) / fd[:, None], "e4m3")
    draftp = pack_weight(n((D, U)) / fd[:, None], "e2m1")
    archp = pack_weight(n((D, X)) / fd[:, None], "e4m3")
    return {
        "query": (n((D, Q)) * 1.0 / np.sqrt(D) * fd[:, None]).astype(np.float32),
        "cache_words": cachep[0],
        "cache_scales": cachep[1],
        "draft_words": draftp[0],
        "draft_scales": draftp[1],
        "arch_words": archp[0],
        "arch_scales": archp[1],
        "offs": striped8(idx),
        "offs2": striped8(idx2),
        "offs3": striped8(idx3),
        "offs4": striped8(idx4),
        "offs5": striped8(idx5),
        "offs6": striped8(idx6),
    }


def reference(query, cache_words, cache_scales, draft_words, draft_scales, arch_words, arch_scales, offs, offs2, offs3, offs4, offs5, offs6):
    idx = unstriped8(offs)
    idx2 = unstriped8(offs2)
    idx3 = unstriped8(offs3)
    idx4 = unstriped8(offs4)
    idx5 = unstriped8(offs5)
    idx6 = unstriped8(offs6)
    cacheu = unpack_weight(cache_words, cache_scales, "e4m3")
    draftu = unpack_weight(draft_words, draft_scales, "e2m1")
    archu = unpack_weight(arch_words, arch_scales, "e4m3")
    queryq = mxq(f64(query), 0, "e4m3")
    a = queryq.T @ cacheu
    b = queryq.T @ draftu
    c0 = queryq.T @ archu
    w = pick8(a, idx, 16) - pick8(b, idx2, 16)
    cl = np.max(w, axis=1, keepdims=True) * 0.25
    v = np.maximum(w, cl)
    f1 = np.zeros((Q, X))
    f1[np.arange(Q)[:, None], idx3[np.arange(Q) % 128 // 16]] = v
    cc = c0 + f1
    r = pick8(cc, idx4, 16) - w
    f2 = np.zeros((Q, T))
    f2[np.arange(Q)[:, None], idx5[np.arange(Q) % 128 // 16]] = r
    aa = a - f2
    y = np.maximum(pick8(aa, idx6, 16), pick8(b, idx2, 16))
    return y

@@ -1,0 +1,150 @@
+from contextlib import ExitStack
+
+import concourse.mybir as mybir
+
+F32 = mybir.dt.float32
+BF16 = mybir.dt.bfloat16
+I32 = mybir.dt.int32
+U32 = mybir.dt.uint32
+U16 = mybir.dt.uint16
+U8 = mybir.dt.uint8
+FP8X4 = mybir.dt.float8_e4m3fn_x4
+FP4X4 = mybir.dt.float4_e2m1fn_x4
+ALU = mybir.AluOpType
+COPY = mybir.ActivationFunctionType.Copy
+
+P = 128
+D, TOKENS, SLOTS, Q = 512, 1024, 512, 128
+PACK = 4
+CHUNK = 256
+BANK = 512
+HALF = SLOTS // 2
+FLOPS = 3 * 2 * D * Q * TOKENS
+
+
+def tile_attend_overbar_three_kernel(
+    tc, query, cache_words, cache_scales, draft_words, draft_scales, arch_words, arch_scales,
+    offs, offs2, offs3, offs4, offs5, offs6, out,
+):
+    nc = tc.nc
+    with ExitStack() as ctx:
+        lists = ctx.enter_context(tc.tile_pool(name="lists", bufs=1))
+        sb = ctx.enter_context(tc.tile_pool(name="sb", bufs=1))
+        psum = ctx.enter_context(tc.psum_pool(name="psum", bufs=1))
+
+        draft_plane = sb.tile([P, TOKENS], U8, align_bytes=64)
+        cache_plane = sb.tile([P, TOKENS], U8, align_bytes=64)
+        arch_plane = sb.tile([P, TOKENS], U8, align_bytes=64)
+        f1 = sb.tile([P, TOKENS], F32)
+        nc.vector.memset(draft_plane[:].bitcast(I32), 0)
+        nc.vector.memset(cache_plane[:].bitcast(I32), 0)
+        nc.vector.memset(arch_plane[:].bitcast(I32), 0)
+        nc.vector.memset(f1[:], 0.0)
+
+        q_raw = sb.tile([P, PACK, Q], F32)
+        draft = sb.tile([P, 2 * TOKENS], U8, align_bytes=64)
+        cache = sb.tile([P, TOKENS], I32, align_bytes=64)
+        arch = sb.tile([P, TOKENS], I32, align_bytes=64)
+        draft_rows = sb.tile([4, 4, TOKENS // 4], I32)
+        cache_rows = sb.tile([4, 4, TOKENS // 4], I32)
+        nc.scalar.dma_start(draft_rows[:], draft_scales[0].bitcast(I32).rearrange("(g r) c -> r g c", r=4))
+        nc.sync.dma_start(q_raw[:], query.rearrange("(p j) w -> p j w", j=PACK))
+        nc.sync.dma_start(draft[:].bitcast(I32), draft_words[0].bitcast(I32))
+        nc.scalar.dma_start(cache_rows[:], cache_scales[0].bitcast(I32).rearrange("(g r) c -> r g c", r=4))
+        nc.sync.dma_start(cache[:], cache_words[0].rearrange("p n t -> p (n t)").bitcast(I32))
+
+        def spread(plane, rows):
+            for g in range(4):
+                nc.vector.tensor_copy(plane[32 * g : 32 * g + 4, :].bitcast(I32), rows[:, g, :])
+
+        def load_list(source, name):
+            tile = lists.tile([P, SLOTS // 16], U16, name=name)
+            nc.sync.dma_start(tile[:], source)
+            return tile
+
+        l2 = load_list(offs2, "l2")
+        l1 = load_list(offs, "l1")
+        l3 = load_list(offs3, "l3")
+        nc.sync.dma_start(arch[:], arch_words[0].rearrange("p n t -> p (n t)").bitcast(I32))
+        for g in range(4):
+            nc.sync.dma_start(arch_plane[32 * g : 32 * g + 4, :].bitcast(I32), arch_scales[0, 4 * g : 4 * g + 4, :].bitcast(I32))
+        l4 = load_list(offs4, "l4")
+        l5 = load_list(offs5, "l5")
+        l6 = load_list(offs6, "l6")
+
+        q_bf = sb.tile([P, Q, PACK], BF16, align_bytes=64)
+        q_codes = sb.tile([P, Q], U32, align_bytes=64)
+        q_plane = sb.tile([P, Q], U8, align_bytes=64)
+        spread(draft_plane, draft_rows)
+        nc.vector.tensor_copy(q_bf[:], q_raw[:].rearrange("p j w -> p w j"))
+        nc.vector.quantize_mx(q_codes[:].bitcast(FP8X4), q_plane[:], q_bf[:].rearrange("p w j -> p (w j)"))
+        spread(cache_plane, cache_rows)
+
+        banks = [psum.tile([P, BANK], F32, name="bank%d" % i) for i in range(8)]
+
+        def score(acc, keys, plane):
+            nc.tensor.matmul_mx(acc, q_codes[:].bitcast(FP8X4), q_plane[:], keys, plane, start=True, stop=True)
+
+        a = sb.tile([P, TOKENS], F32)
+        b = sb.tile([P, TOKENS], F32, tag="b")
+        for i in range(4):
+            cols = slice(i * CHUNK, (i + 1) * CHUNK)
+            acc = banks[i][:, 0:CHUNK]
+            score(acc, draft[:, 2 * i * CHUNK : 2 * (i + 1) * CHUNK].bitcast(FP4X4), draft_plane[:, cols])
+            if i % 2 == 0:
+                nc.scalar.activation(b[:, cols], acc, COPY)
+            else:
+                nc.vector.tensor_copy(b[:, cols], acc)
+        for i in range(4):
+            cols = slice(i * CHUNK, (i + 1) * CHUNK)
+            acc = banks[4 + i][:, 0:CHUNK]
+            score(acc, cache[:, cols].bitcast(FP8X4), cache_plane[:, cols])
+            nc.vector.tensor_copy(a[:, cols], acc)
+        for i in range(2):
+            cols = slice(i * BANK, (i + 1) * BANK)
+            score(banks[i][:], arch[:, cols].bitcast(FP8X4), arch_plane[:, cols])
+
+        lo, hi = slice(0, HALF), slice(HALF, SLOTS)
+        lo_l, hi_l = slice(0, HALF // 16), slice(HALF // 16, SLOTS // 16)
+
+        bg = sb.tile([P, SLOTS], F32)
+        nc.scalar.activation(bg[:], b[:].indirect(l2[:]), COPY)
+        w = sb.tile([P, SLOTS], F32)
+        ag_hi = sb.tile([P, HALF], F32, tag="b")
+        nc.vector.tensor_tensor(w[:, lo], a[:].indirect(l1[:, lo_l]), bg[:, lo], ALU.subtract)
+        nc.scalar.activation(ag_hi[:], a[:].indirect(l1[:, hi_l]), COPY)
+        nc.vector.tensor_tensor(w[:, hi], ag_hi[:], bg[:, hi], ALU.subtract)
+        quarter = sb.tile([P, SLOTS], F32)
+        bar_lo = sb.tile([P, 1], F32, tag="lo")
+        bar_hi = sb.tile([P, 1], F32, tag="hi")
+        nc.vector.tensor_scalar(quarter[:, lo], w[:, lo], 0.25, None, ALU.mult, ALU.max, accum_out=bar_lo[:])
+        nc.vector.tensor_scalar(quarter[:, hi], w[:, hi], 0.25, None, ALU.mult, ALU.max, accum_out=bar_hi[:])
+        v = sb.tile([P, SLOTS], F32)
+        nc.vector.tensor_scalar(v[:], w[:], bar_lo[:], bar_hi[:], ALU.max, ALU.max)
+        nc.scalar.activation(f1[:].indirect(l3[:]), v[:], COPY)
+        f2_lo = sb.tile([P, TOKENS], F32, tag="lo")
+        f2_hi = sb.tile([P, TOKENS], F32, tag="hi")
+        nc.vector.memset(f2_lo[:], 0.0)
+        nc.vector.memset(f2_hi[:], 0.0)
+
+        cc = sb.tile([P, TOKENS], F32)
+        for i in range(2):
+            cols = slice(i * BANK, (i + 1) * BANK)
+            nc.vector.tensor_tensor(cc[:, cols], banks[i][:], f1[:, cols], ALU.add)
+        r = sb.tile([P, SLOTS], F32)
+        for cols, cols_l, f2 in ((lo, lo_l, f2_lo), (hi, hi_l, f2_hi)):
+            nc.vector.tensor_tensor(r[:, cols], cc[:].indirect(l4[:, cols_l]), w[:, cols], ALU.subtract)
+            nc.scalar.activation(f2[:].indirect(l5[:, cols_l]), r[:, cols], COPY)
+
+        aa = sb.tile([P, TOKENS], F32)
+        aa_lo = sb.tile([P, TOKENS], F32)
+        nc.vector.tensor_tensor(aa_lo[:], a[:], f2_lo[:], ALU.subtract)
+        nc.vector.tensor_tensor(aa[:], aa_lo[:], f2_hi[:], ALU.subtract)
+        left = sb.tile([P, SLOTS], F32)
+        y = sb.tile([P, SLOTS], F32)
+        nc.vector.tensor_copy(left[:, lo], aa[:].indirect(l6[:, lo_l]))
+        nc.scalar.activation(left[:, hi], aa[:].indirect(l6[:, hi_l]), COPY)
+        nc.vector.tensor_tensor(y[:, hi], left[:, hi], bg[:, hi], ALU.max)
+        nc.sync.dma_start(out[:, hi], y[:, hi])
+        nc.vector.tensor_tensor(y[:, lo], left[:, lo], bg[:, lo], ALU.max)
+        nc.scalar.dma_start(out[:, lo], y[:, lo])

@@ -45,17 +45,22 @@ def tile_attend_overbar_three_kernel(
         draft = sb.tile([P, 2 * TOKENS], U8, align_bytes=64)
         cache = sb.tile([P, TOKENS], I32, align_bytes=64)
         arch = sb.tile([P, TOKENS], I32, align_bytes=64)
-        draft_rows = sb.tile([4, 4, TOKENS // 4], I32)
-        cache_rows = sb.tile([4, 4, TOKENS // 4], I32)
-        nc.scalar.dma_start(draft_rows[:], draft_scales[0].bitcast(I32).rearrange("(g r) c -> r g c", r=4))
+        def load_rows(queues, scales, name):
+            rows = sb.tile([68, 2, TOKENS // 4], I32, name=name)
+            for h, queue in enumerate(queues):
+                queue.dma_start(rows[64 * h : 64 * h + 4], scales[0, 8 * h : 8 * h + 8, :].bitcast(I32).rearrange("(g r) c -> r g c", r=4))
+            return rows
+
+        draft_rows = load_rows((nc.scalar, nc.scalar), draft_scales, "draft_rows")
         nc.sync.dma_start(q_raw[:], query.rearrange("(p j) w -> p j w", j=PACK))
         nc.sync.dma_start(draft[:].bitcast(I32), draft_words[0].bitcast(I32))
-        nc.scalar.dma_start(cache_rows[:], cache_scales[0].bitcast(I32).rearrange("(g r) c -> r g c", r=4))
+        cache_rows = load_rows((nc.scalar, nc.sync), cache_scales, "cache_rows")
         nc.sync.dma_start(cache[:], cache_words[0].rearrange("p n t -> p (n t)").bitcast(I32))
 
         def spread(plane, rows):
             for g in range(4):
-                nc.vector.tensor_copy(plane[32 * g : 32 * g + 4, :].bitcast(I32), rows[:, g, :])
+                first = 64 * (g // 2)
+                nc.vector.tensor_copy(plane[32 * g : 32 * g + 4, :].bitcast(I32), rows[first : first + 4, g % 2, :])
 
         def load_list(source, name):
             tile = lists.tile([P, SLOTS // 16], U16, name=name)
@@ -86,12 +91,12 @@ def tile_attend_overbar_three_kernel(
             nc.tensor.matmul_mx(acc, q_codes[:].bitcast(FP8X4), q_plane[:], keys, plane, start=True, stop=True)
 
         a = sb.tile([P, TOKENS], F32)
-        b = sb.tile([P, TOKENS], F32, tag="b")
+        b = sb.tile([P, TOKENS], F32)
         for i in range(4):
             cols = slice(i * CHUNK, (i + 1) * CHUNK)
             acc = banks[i][:, 0:CHUNK]
             score(acc, draft[:, 2 * i * CHUNK : 2 * (i + 1) * CHUNK].bitcast(FP4X4), draft_plane[:, cols])
-            if i % 2 == 0:
+            if i < 2:
                 nc.scalar.activation(b[:, cols], acc, COPY)
             else:
                 nc.vector.tensor_copy(b[:, cols], acc)
@@ -108,9 +113,10 @@ def tile_attend_overbar_three_kernel(
         lo_l, hi_l = slice(0, HALF // 16), slice(HALF // 16, SLOTS // 16)
 
         bg = sb.tile([P, SLOTS], F32)
-        nc.scalar.activation(bg[:], b[:].indirect(l2[:]), COPY)
+        nc.scalar.activation(bg[:, lo], b[:].indirect(l2[:, lo_l]), COPY)
+        nc.scalar.activation(bg[:, hi], b[:].indirect(l2[:, hi_l]), COPY)
         w = sb.tile([P, SLOTS], F32)
-        ag_hi = sb.tile([P, HALF], F32, tag="b")
+        ag_hi = sb.tile([P, HALF], F32)
         nc.vector.tensor_tensor(w[:, lo], a[:].indirect(l1[:, lo_l]), bg[:, lo], ALU.subtract)
         nc.scalar.activation(ag_hi[:], a[:].indirect(l1[:, hi_l]), COPY)
         nc.vector.tensor_tensor(w[:, hi], ag_hi[:], bg[:, hi], ALU.subtract)

@@ -19,6 +19,7 @@ PACK = 4
 CHUNK = 256
 BANK = 512
 HALF = SLOTS // 2
+POOL_SHARE = 320
 FLOPS = 3 * 2 * D * Q * TOKENS
 
 
@@ -134,9 +135,12 @@ def tile_attend_overbar_three_kernel(
         nc.vector.memset(f2_hi[:], 0.0)
 
         cc = sb.tile([P, TOKENS], F32)
-        for i in range(2):
-            cols = slice(i * BANK, (i + 1) * BANK)
-            nc.vector.tensor_tensor(cc[:, cols], banks[i][:], f1[:, cols], ALU.add)
+        split = TOKENS - POOL_SHARE
+        c_tail = sb.tile([P, POOL_SHARE], F32)
+        nc.vector.tensor_copy(c_tail[:], banks[1][:, split - BANK : BANK])
+        nc.gpsimd.tensor_tensor(cc[:, split:TOKENS], c_tail[:], f1[:, split:TOKENS], ALU.add)
+        nc.vector.tensor_tensor(cc[:, 0:BANK], banks[0][:], f1[:, 0:BANK], ALU.add)
+        nc.vector.tensor_tensor(cc[:, BANK:split], banks[1][:, 0 : split - BANK], f1[:, BANK:split], ALU.add)
         r = sb.tile([P, SLOTS], F32)
         for cols, cols_l, f2 in ((lo, lo_l, f2_lo), (hi, hi_l, f2_hi)):
             nc.vector.tensor_tensor(r[:, cols], cc[:].indirect(l4[:, cols_l]), w[:, cols], ALU.subtract)
@@ -151,6 +155,6 @@ def tile_attend_overbar_three_kernel(
         nc.vector.tensor_copy(left[:, lo], aa[:].indirect(l6[:, lo_l]))
         nc.scalar.activation(left[:, hi], aa[:].indirect(l6[:, hi_l]), COPY)
         nc.vector.tensor_tensor(y[:, hi], left[:, hi], bg[:, hi], ALU.max)
-        nc.sync.dma_start(out[:, hi], y[:, hi])
+        nc.scalar.dma_start(out[:, hi], y[:, hi])
         nc.vector.tensor_tensor(y[:, lo], left[:, lo], bg[:, lo], ALU.max)
-        nc.scalar.dma_start(out[:, lo], y[:, lo])
+        nc.sync.dma_start(out[:, lo], y[:, lo])

@@ -16,10 +16,13 @@ COPY = mybir.ActivationFunctionType.Copy
 P = 128
 D, TOKENS, SLOTS, Q = 512, 1024, 512, 128
 PACK = 4
-CHUNK = 256
+QUADRANT = 32
+SCALE_ROWS = 4
 BANK = 512
+CHUNK = 256
+B_ON_SCALAR = 2
 HALF = SLOTS // 2
-POOL_SHARE = 320
+POOL_SHARE = 288
 FLOPS = 3 * 2 * D * Q * TOKENS
 
 
@@ -46,22 +49,31 @@ def tile_attend_overbar_three_kernel(
         draft = sb.tile([P, 2 * TOKENS], U8, align_bytes=64)
         cache = sb.tile([P, TOKENS], I32, align_bytes=64)
         arch = sb.tile([P, TOKENS], I32, align_bytes=64)
+
         def load_rows(queues, scales, name):
-            rows = sb.tile([68, 2, TOKENS // 4], I32, name=name)
+            rows = sb.tile([2 * QUADRANT + SCALE_ROWS, 2, TOKENS // 4], I32, name=name)
             for h, queue in enumerate(queues):
-                queue.dma_start(rows[64 * h : 64 * h + 4], scales[0, 8 * h : 8 * h + 8, :].bitcast(I32).rearrange("(g r) c -> r g c", r=4))
+                first = 2 * QUADRANT * h
+                pair = scales[0, 2 * SCALE_ROWS * h : 2 * SCALE_ROWS * (h + 1), :].bitcast(I32)
+                queue.dma_start(rows[first : first + SCALE_ROWS], pair.rearrange("(j r) c -> r j c", r=SCALE_ROWS))
             return rows
 
-        draft_rows = load_rows((nc.scalar, nc.scalar), draft_scales, "draft_rows")
+        draft_rows = load_rows((nc.scalar, nc.sync), draft_scales, "draft_rows")
         nc.sync.dma_start(q_raw[:], query.rearrange("(p j) w -> p j w", j=PACK))
+        cache_rows = load_rows((nc.scalar, nc.scalar), cache_scales, "cache_rows")
         nc.sync.dma_start(draft[:].bitcast(I32), draft_words[0].bitcast(I32))
-        cache_rows = load_rows((nc.scalar, nc.sync), cache_scales, "cache_rows")
-        nc.sync.dma_start(cache[:], cache_words[0].rearrange("p n t -> p (n t)").bitcast(I32))
+        cache_hbm = cache_words[0].rearrange("p n t -> p (n t)").bitcast(I32)
+        for h in range(2):
+            cols = slice(h * TOKENS // 2, (h + 1) * TOKENS // 2)
+            nc.sync.dma_start(cache[:, cols], cache_hbm[:, cols])
 
         def spread(plane, rows):
-            for g in range(4):
-                first = 64 * (g // 2)
-                nc.vector.tensor_copy(plane[32 * g : 32 * g + 4, :].bitcast(I32), rows[first : first + 4, g % 2, :])
+            for g in range(P // QUADRANT):
+                first = 2 * QUADRANT * (g // 2)
+                nc.vector.tensor_copy(
+                    plane[QUADRANT * g : QUADRANT * g + SCALE_ROWS, :].bitcast(I32),
+                    rows[first : first + SCALE_ROWS, g % 2, :],
+                )
 
         def load_list(source, name):
             tile = lists.tile([P, SLOTS // 16], U16, name=name)
@@ -69,11 +81,14 @@ def tile_attend_overbar_three_kernel(
             return tile
 
         l2 = load_list(offs2, "l2")
-        l1 = load_list(offs, "l1")
         l3 = load_list(offs3, "l3")
+        l1 = load_list(offs, "l1")
         nc.sync.dma_start(arch[:], arch_words[0].rearrange("p n t -> p (n t)").bitcast(I32))
-        for g in range(4):
-            nc.sync.dma_start(arch_plane[32 * g : 32 * g + 4, :].bitcast(I32), arch_scales[0, 4 * g : 4 * g + 4, :].bitcast(I32))
+        for g in range(P // QUADRANT):
+            nc.sync.dma_start(
+                arch_plane[QUADRANT * g : QUADRANT * g + SCALE_ROWS, :].bitcast(I32),
+                arch_scales[0, SCALE_ROWS * g : SCALE_ROWS * (g + 1), :].bitcast(I32),
+            )
         l4 = load_list(offs4, "l4")
         l5 = load_list(offs5, "l5")
         l6 = load_list(offs6, "l6")
@@ -87,40 +102,42 @@ def tile_attend_overbar_three_kernel(
         spread(cache_plane, cache_rows)
 
         banks = [psum.tile([P, BANK], F32, name="bank%d" % i) for i in range(8)]
+        chunks = TOKENS // CHUNK
 
         def score(acc, keys, plane):
             nc.tensor.matmul_mx(acc, q_codes[:].bitcast(FP8X4), q_plane[:], keys, plane, start=True, stop=True)
 
         a = sb.tile([P, TOKENS], F32)
         b = sb.tile([P, TOKENS], F32)
-        for i in range(4):
+        for i in range(chunks):
             cols = slice(i * CHUNK, (i + 1) * CHUNK)
             acc = banks[i][:, 0:CHUNK]
             score(acc, draft[:, 2 * i * CHUNK : 2 * (i + 1) * CHUNK].bitcast(FP4X4), draft_plane[:, cols])
-            if i < 2:
+            if i < B_ON_SCALAR:
                 nc.scalar.activation(b[:, cols], acc, COPY)
             else:
                 nc.vector.tensor_copy(b[:, cols], acc)
-        for i in range(4):
+        for i in range(chunks):
             cols = slice(i * CHUNK, (i + 1) * CHUNK)
-            acc = banks[4 + i][:, 0:CHUNK]
+            acc = banks[chunks + i][:, 0:CHUNK]
             score(acc, cache[:, cols].bitcast(FP8X4), cache_plane[:, cols])
             nc.vector.tensor_copy(a[:, cols], acc)
-        for i in range(2):
+        for i in range(TOKENS // BANK):
             cols = slice(i * BANK, (i + 1) * BANK)
             score(banks[i][:], arch[:, cols].bitcast(FP8X4), arch_plane[:, cols])
 
         lo, hi = slice(0, HALF), slice(HALF, SLOTS)
         lo_l, hi_l = slice(0, HALF // 16), slice(HALF // 16, SLOTS // 16)
 
-        bg = sb.tile([P, SLOTS], F32)
-        nc.scalar.activation(bg[:, lo], b[:].indirect(l2[:, lo_l]), COPY)
-        nc.scalar.activation(bg[:, hi], b[:].indirect(l2[:, hi_l]), COPY)
+        b_picked = sb.tile([P, SLOTS], F32)
+        nc.scalar.activation(b_picked[:, lo], b[:].indirect(l2[:, lo_l]), COPY)
+        nc.scalar.activation(b_picked[:, hi], b[:].indirect(l2[:, hi_l]), COPY)
         w = sb.tile([P, SLOTS], F32)
-        ag_hi = sb.tile([P, HALF], F32)
-        nc.vector.tensor_tensor(w[:, lo], a[:].indirect(l1[:, lo_l]), bg[:, lo], ALU.subtract)
-        nc.scalar.activation(ag_hi[:], a[:].indirect(l1[:, hi_l]), COPY)
-        nc.vector.tensor_tensor(w[:, hi], ag_hi[:], bg[:, hi], ALU.subtract)
+        a_picked_hi = sb.tile([P, HALF], F32)
+        nc.vector.tensor_tensor(w[:, lo], a[:].indirect(l1[:, lo_l]), b_picked[:, lo], ALU.subtract)
+        nc.scalar.activation(a_picked_hi[:], a[:].indirect(l1[:, hi_l]), COPY)
+        nc.vector.tensor_tensor(w[:, hi], a_picked_hi[:], b_picked[:, hi], ALU.subtract)
+
         quarter = sb.tile([P, SLOTS], F32)
         bar_lo = sb.tile([P, 1], F32, tag="lo")
         bar_hi = sb.tile([P, 1], F32, tag="hi")
@@ -129,6 +146,7 @@ def tile_attend_overbar_three_kernel(
         v = sb.tile([P, SLOTS], F32)
         nc.vector.tensor_scalar(v[:], w[:], bar_lo[:], bar_hi[:], ALU.max, ALU.max)
         nc.scalar.activation(f1[:].indirect(l3[:]), v[:], COPY)
+
         f2_lo = sb.tile([P, TOKENS], F32, tag="lo")
         f2_hi = sb.tile([P, TOKENS], F32, tag="hi")
         nc.vector.memset(f2_lo[:], 0.0)
@@ -141,20 +159,22 @@ def tile_attend_overbar_three_kernel(
         nc.gpsimd.tensor_tensor(cc[:, split:TOKENS], c_tail[:], f1[:, split:TOKENS], ALU.add)
         nc.vector.tensor_tensor(cc[:, 0:BANK], banks[0][:], f1[:, 0:BANK], ALU.add)
         nc.vector.tensor_tensor(cc[:, BANK:split], banks[1][:, 0 : split - BANK], f1[:, BANK:split], ALU.add)
+
         r = sb.tile([P, SLOTS], F32)
         for cols, cols_l, f2 in ((lo, lo_l, f2_lo), (hi, hi_l, f2_hi)):
             nc.vector.tensor_tensor(r[:, cols], cc[:].indirect(l4[:, cols_l]), w[:, cols], ALU.subtract)
             nc.scalar.activation(f2[:].indirect(l5[:, cols_l]), r[:, cols], COPY)
 
         aa = sb.tile([P, TOKENS], F32)
-        aa_lo = sb.tile([P, TOKENS], F32)
-        nc.vector.tensor_tensor(aa_lo[:], a[:], f2_lo[:], ALU.subtract)
-        nc.vector.tensor_tensor(aa[:], aa_lo[:], f2_hi[:], ALU.subtract)
-        left = sb.tile([P, SLOTS], F32)
+        aa_part = sb.tile([P, TOKENS], F32)
+        nc.vector.tensor_tensor(aa_part[:], a[:], f2_lo[:], ALU.subtract)
+        nc.vector.tensor_tensor(aa[:], aa_part[:], f2_hi[:], ALU.subtract)
+
+        aa_picked = sb.tile([P, SLOTS], F32)
         y = sb.tile([P, SLOTS], F32)
-        nc.vector.tensor_copy(left[:, lo], aa[:].indirect(l6[:, lo_l]))
-        nc.scalar.activation(left[:, hi], aa[:].indirect(l6[:, hi_l]), COPY)
-        nc.vector.tensor_tensor(y[:, hi], left[:, hi], bg[:, hi], ALU.max)
+        nc.vector.tensor_copy(aa_picked[:, lo], aa[:].indirect(l6[:, lo_l]))
+        nc.scalar.activation(aa_picked[:, hi], aa[:].indirect(l6[:, hi_l]), COPY)
+        nc.vector.tensor_tensor(y[:, hi], aa_picked[:, hi], b_picked[:, hi], ALU.max)
         nc.scalar.dma_start(out[:, hi], y[:, hi])
-        nc.vector.tensor_tensor(y[:, lo], left[:, lo], bg[:, lo], ALU.max)
+        nc.vector.tensor_tensor(y[:, lo], aa_picked[:, lo], b_picked[:, lo], ALU.max)
         nc.sync.dma_start(out[:, lo], y[:, lo])

from contextlib import ExitStack

import concourse.mybir as mybir

F32 = mybir.dt.float32
BF16 = mybir.dt.bfloat16
I32 = mybir.dt.int32
U32 = mybir.dt.uint32
U16 = mybir.dt.uint16
U8 = mybir.dt.uint8
FP8X4 = mybir.dt.float8_e4m3fn_x4
FP4X4 = mybir.dt.float4_e2m1fn_x4
ALU = mybir.AluOpType
COPY = mybir.ActivationFunctionType.Copy

P = 128
D, TOKENS, SLOTS, Q = 512, 1024, 512, 128
PACK = 4
QUADRANT = 32
SCALE_ROWS = 4
BANK = 512
CHUNK = 256
B_ON_SCALAR = 2
HALF = SLOTS // 2
POOL_SHARE = 288
FLOPS = 3 * 2 * D * Q * TOKENS


def tile_attend_overbar_three_kernel(
    tc, query, cache_words, cache_scales, draft_words, draft_scales, arch_words, arch_scales,
    offs, offs2, offs3, offs4, offs5, offs6, out,
):
    nc = tc.nc
    with ExitStack() as ctx:
        lists = ctx.enter_context(tc.tile_pool(name="lists", bufs=1))
        sb = ctx.enter_context(tc.tile_pool(name="sb", bufs=1))
        psum = ctx.enter_context(tc.psum_pool(name="psum", bufs=1))

        draft_plane = sb.tile([P, TOKENS], U8, align_bytes=64)
        cache_plane = sb.tile([P, TOKENS], U8, align_bytes=64)
        arch_plane = sb.tile([P, TOKENS], U8, align_bytes=64)
        f1 = sb.tile([P, TOKENS], F32)
        nc.vector.memset(draft_plane[:].bitcast(I32), 0)
        nc.vector.memset(cache_plane[:].bitcast(I32), 0)
        nc.vector.memset(arch_plane[:].bitcast(I32), 0)
        nc.vector.memset(f1[:], 0.0)

        q_raw = sb.tile([P, PACK, Q], F32)
        draft = sb.tile([P, 2 * TOKENS], U8, align_bytes=64)
        cache = sb.tile([P, TOKENS], I32, align_bytes=64)
        arch = sb.tile([P, TOKENS], I32, align_bytes=64)

        def load_rows(queues, scales, name):
            rows = sb.tile([2 * QUADRANT + SCALE_ROWS, 2, TOKENS // 4], I32, name=name)
            for h, queue in enumerate(queues):
                first = 2 * QUADRANT * h
                pair = scales[0, 2 * SCALE_ROWS * h : 2 * SCALE_ROWS * (h + 1), :].bitcast(I32)
                queue.dma_start(rows[first : first + SCALE_ROWS], pair.rearrange("(j r) c -> r j c", r=SCALE_ROWS))
            return rows

        draft_rows = load_rows((nc.scalar, nc.sync), draft_scales, "draft_rows")
        nc.sync.dma_start(q_raw[:], query.rearrange("(p j) w -> p j w", j=PACK))
        cache_rows = load_rows((nc.scalar, nc.scalar), cache_scales, "cache_rows")
        nc.sync.dma_start(draft[:].bitcast(I32), draft_words[0].bitcast(I32))
        cache_hbm = cache_words[0].rearrange("p n t -> p (n t)").bitcast(I32)
        for h in range(2):
            cols = slice(h * TOKENS // 2, (h + 1) * TOKENS // 2)
            nc.sync.dma_start(cache[:, cols], cache_hbm[:, cols])

        def spread(plane, rows):
            for g in range(P // QUADRANT):
                first = 2 * QUADRANT * (g // 2)
                nc.vector.tensor_copy(
                    plane[QUADRANT * g : QUADRANT * g + SCALE_ROWS, :].bitcast(I32),
                    rows[first : first + SCALE_ROWS, g % 2, :],
                )

        def load_list(source, name):
            tile = lists.tile([P, SLOTS // 16], U16, name=name)
            nc.sync.dma_start(tile[:], source)
            return tile

        l2 = load_list(offs2, "l2")
        l3 = load_list(offs3, "l3")
        l1 = load_list(offs, "l1")
        nc.sync.dma_start(arch[:], arch_words[0].rearrange("p n t -> p (n t)").bitcast(I32))
        for g in range(P // QUADRANT):
            nc.sync.dma_start(
                arch_plane[QUADRANT * g : QUADRANT * g + SCALE_ROWS, :].bitcast(I32),
                arch_scales[0, SCALE_ROWS * g : SCALE_ROWS * (g + 1), :].bitcast(I32),
            )
        l4 = load_list(offs4, "l4")
        l5 = load_list(offs5, "l5")
        l6 = load_list(offs6, "l6")

        q_bf = sb.tile([P, Q, PACK], BF16, align_bytes=64)
        q_codes = sb.tile([P, Q], U32, align_bytes=64)
        q_plane = sb.tile([P, Q], U8, align_bytes=64)
        spread(draft_plane, draft_rows)
        nc.vector.tensor_copy(q_bf[:], q_raw[:].rearrange("p j w -> p w j"))
        nc.vector.quantize_mx(q_codes[:].bitcast(FP8X4), q_plane[:], q_bf[:].rearrange("p w j -> p (w j)"))
        spread(cache_plane, cache_rows)

        banks = [psum.tile([P, BANK], F32, name="bank%d" % i) for i in range(8)]
        chunks = TOKENS // CHUNK

        def score(acc, keys, plane):
            nc.tensor.matmul_mx(acc, q_codes[:].bitcast(FP8X4), q_plane[:], keys, plane, start=True, stop=True)

        a = sb.tile([P, TOKENS], F32)
        b = sb.tile([P, TOKENS], F32)
        for i in range(chunks):
            cols = slice(i * CHUNK, (i + 1) * CHUNK)
            acc = banks[i][:, 0:CHUNK]
            score(acc, draft[:, 2 * i * CHUNK : 2 * (i + 1) * CHUNK].bitcast(FP4X4), draft_plane[:, cols])
            if i < B_ON_SCALAR:
                nc.scalar.activation(b[:, cols], acc, COPY)
            else:
                nc.vector.tensor_copy(b[:, cols], acc)
        for i in range(chunks):
            cols = slice(i * CHUNK, (i + 1) * CHUNK)
            acc = banks[chunks + i][:, 0:CHUNK]
            score(acc, cache[:, cols].bitcast(FP8X4), cache_plane[:, cols])
            nc.vector.tensor_copy(a[:, cols], acc)
        for i in range(TOKENS // BANK):
            cols = slice(i * BANK, (i + 1) * BANK)
            score(banks[i][:], arch[:, cols].bitcast(FP8X4), arch_plane[:, cols])

        lo, hi = slice(0, HALF), slice(HALF, SLOTS)
        lo_l, hi_l = slice(0, HALF // 16), slice(HALF // 16, SLOTS // 16)

        b_picked = sb.tile([P, SLOTS], F32)
        nc.scalar.activation(b_picked[:, lo], b[:].indirect(l2[:, lo_l]), COPY)
        nc.scalar.activation(b_picked[:, hi], b[:].indirect(l2[:, hi_l]), COPY)
        w = sb.tile([P, SLOTS], F32)
        a_picked_hi = sb.tile([P, HALF], F32)
        nc.vector.tensor_tensor(w[:, lo], a[:].indirect(l1[:, lo_l]), b_picked[:, lo], ALU.subtract)
        nc.scalar.activation(a_picked_hi[:], a[:].indirect(l1[:, hi_l]), COPY)
        nc.vector.tensor_tensor(w[:, hi], a_picked_hi[:], b_picked[:, hi], ALU.subtract)

        quarter = sb.tile([P, SLOTS], F32)
        bar_lo = sb.tile([P, 1], F32, tag="lo")
        bar_hi = sb.tile([P, 1], F32, tag="hi")
        nc.vector.tensor_scalar(quarter[:, lo], w[:, lo], 0.25, None, ALU.mult, ALU.max, accum_out=bar_lo[:])
        nc.vector.tensor_scalar(quarter[:, hi], w[:, hi], 0.25, None, ALU.mult, ALU.max, accum_out=bar_hi[:])
        v = sb.tile([P, SLOTS], F32)
        nc.vector.tensor_scalar(v[:], w[:], bar_lo[:], bar_hi[:], ALU.max, ALU.max)
        nc.scalar.activation(f1[:].indirect(l3[:]), v[:], COPY)

        f2_lo = sb.tile([P, TOKENS], F32, tag="lo")
        f2_hi = sb.tile([P, TOKENS], F32, tag="hi")
        nc.vector.memset(f2_lo[:], 0.0)
        nc.vector.memset(f2_hi[:], 0.0)

        cc = sb.tile([P, TOKENS], F32)
        split = TOKENS - POOL_SHARE
        c_tail = sb.tile([P, POOL_SHARE], F32)
        nc.vector.tensor_copy(c_tail[:], banks[1][:, split - BANK : BANK])
        nc.gpsimd.tensor_tensor(cc[:, split:TOKENS], c_tail[:], f1[:, split:TOKENS], ALU.add)
        nc.vector.tensor_tensor(cc[:, 0:BANK], banks[0][:], f1[:, 0:BANK], ALU.add)
        nc.vector.tensor_tensor(cc[:, BANK:split], banks[1][:, 0 : split - BANK], f1[:, BANK:split], ALU.add)

        r = sb.tile([P, SLOTS], F32)
        for cols, cols_l, f2 in ((lo, lo_l, f2_lo), (hi, hi_l, f2_hi)):
            nc.vector.tensor_tensor(r[:, cols], cc[:].indirect(l4[:, cols_l]), w[:, cols], ALU.subtract)
            nc.scalar.activation(f2[:].indirect(l5[:, cols_l]), r[:, cols], COPY)

        aa = sb.tile([P, TOKENS], F32)
        aa_part = sb.tile([P, TOKENS], F32)
        nc.vector.tensor_tensor(aa_part[:], a[:], f2_lo[:], ALU.subtract)
        nc.vector.tensor_tensor(aa[:], aa_part[:], f2_hi[:], ALU.subtract)

        aa_picked = sb.tile([P, SLOTS], F32)
        y = sb.tile([P, SLOTS], F32)
        nc.vector.tensor_copy(aa_picked[:, lo], aa[:].indirect(l6[:, lo_l]))
        nc.scalar.activation(aa_picked[:, hi], aa[:].indirect(l6[:, hi_l]), COPY)
        nc.vector.tensor_tensor(y[:, hi], aa_picked[:, hi], b_picked[:, hi], ALU.max)
        nc.scalar.dma_start(out[:, hi], y[:, hi])
        nc.vector.tensor_tensor(y[:, lo], aa_picked[:, lo], b_picked[:, lo], ALU.max)
        nc.sync.dma_start(out[:, lo], y[:, lo])
